import numpy as np
import ml_dtypes


def mxq(x, axis, fmt="e4m3"):
    dtype, down = {"e4m3": (ml_dtypes.float8_e4m3fn, 7), "e5m2": (ml_dtypes.float8_e5m2, 14)}[fmt]
    v = np.moveaxis(np.asarray(x, np.float32).astype(ml_dtypes.bfloat16).astype(np.float64), axis, -1)
    blocks = v.reshape(v.shape[:-1] + (-1, 32))
    amax = np.abs(blocks).max(-1, keepdims=True)
    byte = np.maximum(np.where(amax > 0, np.frexp(amax)[1] - 1 + 127, 0) - down, 1)
    scale = np.exp2(byte - 127.0)
    codes = (blocks / scale).astype(np.float32).astype(dtype).astype(np.float64)
    return np.moveaxis((codes * scale).reshape(v.shape), -1, axis)


WIDE = False


def mx_kscale(k):
    if not WIDE:
        return np.ones(k)
    levels = np.array([10, -10, 5, -5, 0])
    if k % 512:
        return np.exp2(np.random.permutation(np.resize(levels, k // 32))).repeat(32)
    a = np.empty((k // 512, 16))
    for p in range(k // 512):
        a[p, :8] = np.random.permutation(np.resize(levels, 8))
        for g in range(8):
            far = levels[np.abs(levels - a[p, g]) >= 10]
            a[p, g + 8] = far[np.random.randint(len(far))]
    return np.exp2(a.ravel()).repeat(32)


def f64(x):
    return np.asarray(x).astype(np.float64)


def striped(idx):
    return np.tile(idx.reshape(-1, 16).T, (8, 1)).astype(np.uint16)


def unstriped(offs):
    return offs[:16].T.reshape(-1).astype(np.int64)


def striped8(idx):
    return np.concatenate([x.reshape(-1, 16).T for x in idx]).astype(np.uint16)


def runs(offs, k):
    lists = np.stack([offs[16 * r : 16 * r + 16].T.reshape(-1) for r in range(8)]).astype(np.int64)
    return lists[np.arange(k) % 512 // 64]


def pack_weight(w):
    k, n = w.shape
    w = f64(np.asarray(w, np.float32).astype(ml_dtypes.bfloat16)).reshape(k // 32, 32, n)
    amax = np.abs(w).max(1)
    byte = np.clip(np.where(amax > 0, np.frexp(amax)[1] - 1 + 127 - 7, 1), 1, 254)
    scaled = (w * np.exp2(127.0 - byte)[:, None, :]).reshape(k, n).astype(np.float32)
    words = np.ascontiguousarray(scaled.reshape(k // 512, 128, 4, n).transpose(0, 1, 3, 2)).astype(ml_dtypes.float8_e4m3fn).view(np.uint8)
    return words, np.ascontiguousarray(byte.astype(np.uint8).reshape(k // 512, 16, n))


def unpack_weight(words, scales):
    g, p, n, _ = words.shape
    vals = np.ascontiguousarray(words).view(ml_dtypes.float8_e4m3fn).astype(np.float64) * np.repeat(np.exp2(scales.astype(np.float64) - 127.0), 8, axis=1)[..., None]
    return vals.transpose(0, 1, 3, 2).reshape(g * 512, n)


E2M1 = np.array([0.0, 0.5, 1.0, 1.5, 2.0, 3.0, 4.0, 6.0, -0.0, -0.5, -1.0, -1.5, -2.0, -3.0, -4.0, -6.0])


def pack_fp4(w):
    k, n = w.shape
    w = f64(np.asarray(w, np.float32).astype(ml_dtypes.bfloat16)).reshape(k // 32, 32, n)
    amax = np.abs(w).max(1)
    mant, ex = np.frexp(amax / 6.0)
    byte = np.clip(np.where(amax > 0, np.where(mant > 0.5, ex, ex - 1) + 127, 1), 1, 254)
    scaled = (w * np.exp2(127.0 - byte)[:, None, :]).reshape(k, n).astype(np.float32)
    c = np.ascontiguousarray(scaled.reshape(k // 512, 128, 4, n).transpose(0, 1, 3, 2)).astype(ml_dtypes.float4_e2m1fn).view(np.uint8) & 0xF
    words = (c[..., 0::2] | (c[..., 1::2] << 4)).reshape(k // 512, 128, 2 * n)
    return np.ascontiguousarray(words), np.ascontiguousarray(byte.astype(np.uint8).reshape(k // 512, 16, n))


def unpack_fp4(words, scales):
    g, _, n = scales.shape
    words = np.ascontiguousarray(words).reshape(g, 128, n, 2)
    nib = np.empty((g, 128, n, 4), np.uint8)
    nib[..., 0::2] = words & 0xF
    nib[..., 1::2] = words >> 4
    vals = E2M1[nib] * np.repeat(np.exp2(scales.astype(np.float64) - 127.0), 8, axis=1)[..., None]
    return vals.transpose(0, 1, 3, 2).reshape(g * 512, n)


def planes(y):
    n, m = y.shape
    v = y.astype(np.float32).astype(ml_dtypes.bfloat16).astype(np.float64).reshape(n // 32, 32, m)
    top = np.abs(v).max(1)
    byte = np.clip(np.where(top > 0, np.frexp(top)[1] - 1 + 127 - 7, 1), 1, 254)
    codes = (v * np.exp2(127.0 - byte)[:, None, :]).reshape(n, m).astype(np.float32).astype(ml_dtypes.float8_e4m3fn).view(np.uint8)
    words = codes.reshape(n // 512, 128, 4, m).transpose(0, 1, 3, 2)
    return np.ascontiguousarray(words), np.ascontiguousarray(byte.astype(np.uint8).reshape(n // 512, 16, m))


K, T, S, H, G, W = 512, 1024, 256, 512, 2048, 192


def setup_inputs():
    n = np.random.standard_normal
    s = mx_kscale(K)[:, None]
    packed_xT = pack_weight(n((K, T)) * s)
    packed_w1 = pack_fp4(n((K, H)) / np.sqrt(K) / s)
    packed_w2 = pack_fp4(n((K, H)) / np.sqrt(K) / s)
    packed_dT = pack_weight(n((K, G)) / s)
    return {
        "x_words": packed_xT[0],
        "x_scales": packed_xT[1],
        "w1_words": packed_w1[0],
        "w1_scales": packed_w1[1],
        "w2_words": packed_w2[0],
        "w2_scales": packed_w2[1],
        "gs": (np.random.uniform(0.5, 1.5, (K, 1)) * s).astype(np.float32),
        "d_words": packed_dT[0],
        "d_scales": packed_dT[1],
        "offs": striped(np.random.permutation(T)[:S]),
        "two": striped(np.random.permutation(T)[:S]),
        "n1": striped(np.random.permutation(S)),
        "n2": striped(np.random.permutation(S)),
        "k1": striped8(np.random.randint(0, G, (8, H))),
        "n3": striped(np.random.permutation(S)[:W]),
        "n4": striped(np.random.permutation(S)[:W]),
    }


def reference(x_words, x_scales, w1_words, w1_scales, w2_words, w2_scales, gs, d_words, d_scales, offs, two, n1, n2, k1, n3, n4):
    d_k1 = unpack_weight(d_words, d_scales)[np.arange(K)[:, None], runs(k1, K)]
    xq = unpack_weight(x_words, x_scales)[:, unstriped(offs)]
    y = unpack_fp4(w1_words, w1_scales).T @ xq
    x_two = unpack_weight(x_words, x_scales)[:, unstriped(two)]
    d = unpack_fp4(w2_words, w2_scales).T @ x_two
    z = f64(gs) * (y * (np.tanh(d[:, unstriped(n1)] - d[:, unstriped(n2)])))
    h = 0.0625 * ((d_k1.T @ mxq(z, 0, "e4m3")))
    old = h[:, unstriped(n3)]
    pa = h[:, unstriped(n4)]
    ra = old - (0.5 * pa)
    out = h.copy()
    out[:, unstriped(n3)] = ra
    return (out,) + planes(out)

@@ -1,0 +1,232 @@
+from contextlib import ExitStack
+
+import concourse.mybir as mybir
+
+F32 = mybir.dt.float32
+BF16 = mybir.dt.bfloat16
+I32 = mybir.dt.int32
+U32 = mybir.dt.uint32
+U16 = mybir.dt.uint16
+U8 = mybir.dt.uint8
+FP8X4 = mybir.dt.float8_e4m3fn_x4
+FP4X4 = mybir.dt.float4_e2m1fn_x4
+ACT = mybir.ActivationFunctionType
+ALU = mybir.AluOpType
+
+P = 128
+PACK = 4
+TOKENS = 1024
+CODEWORDS = 2048
+FEATURES = 512
+PLACES = 256
+CHANGED = 192
+HALF = PLACES // 2
+LIST_ROWS = 16
+
+FLOPS = 3 * 2 * FEATURES * FEATURES * PLACES
+
+
+def tile_picked_twqjointbkdif_none_po_kernel(
+    tc, x_words, x_scales, w1_words, w1_scales, w2_words, w2_scales, gs, d_words, d_scales,
+    offs, two, n1, n2, k1, n3, n4, out_0, out_1, out_2,
+):
+    nc = tc.nc
+    with ExitStack() as ctx:
+        lists = ctx.enter_context(tc.tile_pool(name="lists", bufs=1))
+        sb = ctx.enter_context(tc.tile_pool(name="sb", bufs=1))
+        ps = ctx.enter_context(tc.psum_pool(name="ps", bufs=1))
+
+        def load_list(src, name):
+            t = lists.tile(list(src.shape), U16, name=name)
+            nc.sync.dma_start(t[:], src)
+            return t
+
+        def zeroed_bytes(width, name, eng):
+            t = sb.tile([P, width], U8, name=name, align_bytes=64)
+            eng.memset(t[:].bitcast(I32), 0)
+            return t
+
+        def load_scale_rows(t, src, queues):
+            for q in range(4):
+                queues[q].dma_start(t[32 * q : 32 * q + 4, :].bitcast(I32), src[0, 4 * q : 4 * q + 4, :].bitcast(I32))
+
+        def words_of(src):
+            return src[0].rearrange("p n t -> p (n t)").bitcast(I32)
+
+        w2s_raw = zeroed_bytes(FEATURES, "w2s_raw", nc.gpsimd)
+        xs_tab = zeroed_bytes(TOKENS, "xs_tab", nc.vector)
+        ds_tab = zeroed_bytes(CODEWORDS, "ds_tab", nc.vector)
+        w1s_raw = zeroed_bytes(FEATURES, "w1s_raw", nc.vector)
+
+        load_scale_rows(xs_tab, x_scales, [nc.sync] * 4)
+        load_scale_rows(w2s_raw, w2_scales, [nc.gpsimd, nc.gpsimd, nc.sync, nc.sync])
+        for e in range(2):
+            nc.gpsimd.dma_start(ds_tab[e:P:16, :].bitcast(I32), d_scales[0, e:16:2, :].bitcast(I32))
+        two_t = load_list(two, "two_t")
+        w2w_raw = sb.tile([P, 2 * FEATURES], U8, name="w2w_raw", align_bytes=64)
+        nc.sync.dma_start(w2w_raw[:].bitcast(I32), w2_words[0].bitcast(I32))
+        offs_t = load_list(offs, "offs_t")
+        n1_t = load_list(n1, "n1_t")
+        n2_t = load_list(n2, "n2_t")
+        k1_t = load_list(k1, "k1_t")
+        xw_tab = sb.tile([P, TOKENS], U32, name="xw_tab", align_bytes=64)
+        nc.sync.dma_start(xw_tab[:].bitcast(I32), words_of(x_words))
+        w1w_raw = sb.tile([P, 2 * FEATURES], U8, name="w1w_raw", align_bytes=64)
+        nc.sync.dma_start(w1w_raw[:].bitcast(I32), w1_words[0].bitcast(I32))
+        dw_tab = sb.tile([P, CODEWORDS], U32, name="dw_tab", align_bytes=64)
+        nc.sync.dma_start(dw_tab[:].bitcast(I32), words_of(d_words))
+        load_scale_rows(w1s_raw, w1_scales, [nc.sync] * 4)
+        gs_t = sb.tile([P, PACK], F32, name="gs_t")
+        nc.sync.dma_start(gs_t[:], gs.rearrange("(p t) o -> p (t o)", t=PACK))
+        n3_t = load_list(n3, "n3_t")
+        n4_t = load_list(n4, "n4_t")
+
+        def gathered(table, offsets, n, dtype, name, tag=None):
+            t = sb.tile([P, n], dtype, name=name, tag=tag or name, align_bytes=64)
+            nc.vector.tensor_copy(t[:], table[:].indirect(offsets[:]))
+            return t
+
+        def dealt(copy, raw, view, name):
+            t = sb.tile(list(raw[:].shape), raw[:].dtype, name=name, align_bytes=64)
+            dst, src = (t[:], raw[:]) if view is None else (t[:].bitcast(view), raw[:].bitcast(view))
+            copy(dst.rearrange("p (t m) -> p m t", t=PACK), src.rearrange("p (m t) -> p m t", t=PACK))
+            return t
+
+        def project(out, w_words, w_scales, t, xw, xs):
+            nc.tensor.matmul_mx(
+                out=out,
+                lhsT=w_words[:, 2 * P * t : 2 * P * (t + 1)].bitcast(FP4X4),
+                lhsT_scale=w_scales[:, P * t : P * (t + 1)],
+                rhs=xw[:].bitcast(FP8X4),
+                rhs_scale=xs[:],
+                start=True,
+                stop=True,
+            )
+
+        xs_two = gathered(xs_tab, two_t, PLACES, U8, "xs_two")
+        w2w = dealt(nc.scalar.copy, w2w_raw, U16, "w2w")
+        w1w = dealt(nc.scalar.copy, w1w_raw, U16, "w1w")
+        xw_two = gathered(xw_tab, two_t, PLACES, U32, "xw_two")
+        w2s = dealt(nc.vector.tensor_copy, w2s_raw, None, "w2s")
+        d_rows = []
+        for t in range(PACK):
+            bank = ps.tile([P, PLACES], F32, name=f"d_bank{t}", tag=f"bank{t}")
+            project(bank[:], w2w, w2s, t, xw_two, xs_two)
+            row = sb.tile([P, PLACES], F32, name=f"d_row{t}")
+            nc.scalar.activation(row[:], bank[:], ACT.Copy)
+            d_rows.append(row)
+
+        xs_idx = gathered(xs_tab, offs_t, PLACES, U8, "xs_idx")
+        xw_idx = gathered(xw_tab, offs_t, PLACES, U32, "xw_idx")
+
+        ds_k1 = gathered(ds_tab, k1_t, FEATURES, U8, "ds_k1", "stage")
+        dks = dealt(nc.vector.tensor_copy, ds_k1, None, "dks")
+        for e in range(2):
+            nc.sync.dma_start(dks[2 + e : P : 32, :].bitcast(I32), dks[16 + e : P : 32, :].bitcast(I32))
+
+        w1s = dealt(nc.vector.tensor_copy, w1s_raw, None, "w1s")
+        y_banks = [ps.tile([P, 2, PLACES], F32, name=f"y_bank{u}") for u in range(2)]
+        for t in range(PACK):
+            project(y_banks[t // 2][:, t % 2, :], w1w, w1s, t, xw_idx, xs_idx)
+
+        dw_k1 = gathered(dw_tab, k1_t, FEATURES, U32, "dw_k1", "stage")
+        dkw = dealt(nc.vector.tensor_copy, dw_k1, None, "dkw")
+
+        h_rows = [sb.tile([P, PLACES], F32, name=f"h_row{t}") for t in range(PACK)]
+        h_first = ps.tile([P, PACK, HALF], F32, name="h_first")
+        z_planes = [sb.tile([P, PACK, HALF], F32, name=f"z_planes{c}") for c in range(2)]
+
+        def fetch(c, offsets, name, tag):
+            entries = slice(c * HALF // LIST_ROWS, (c + 1) * HALF // LIST_ROWS)
+            picked = sb.tile([P, PACK, HALF], F32, name=name, tag=tag, align_bytes=64)
+            for t in range(PACK):
+                nc.scalar.activation(picked[:, t, :], d_rows[t][:].indirect(offsets[:, entries]), ACT.Copy)
+            return picked
+
+        def difference(at_n1, at_n2, ts, name, tag):
+            diff = sb.tile([P, len(ts), HALF], F32, name=name, tag=tag, align_bytes=64)
+            planes = slice(ts[0], ts[-1] + 1)
+            nc.vector.tensor_tensor(diff[:], at_n1[:, planes, :], at_n2[:, planes, :], ALU.subtract)
+            return diff[:]
+
+        def weigh(c, ts, diff):
+            cols = slice(c * HALF, (c + 1) * HALF)
+            gate = sb.tile([P, len(ts), HALF], F32, name=f"gate{c}{ts[0]}")
+            nc.scalar.activation(gate[:], diff, ACT.Tanh)
+            for i, t in enumerate(ts):
+                nc.vector.scalar_tensor_tensor(
+                    z_planes[c][:, t, :], y_banks[t // 2][:, t % 2, cols], gs_t[:, t : t + 1], gate[:, i, :], ALU.mult, ALU.mult
+                )
+
+        def quantised(c):
+            z_bf = sb.tile([P, HALF, PACK], BF16, name=f"z_bf{c}", align_bytes=64)
+            nc.vector.tensor_copy(
+                z_bf[:].rearrange("p (a i) t -> p a t i", i=4), z_planes[c][:].rearrange("p t (a i) -> p a t i", i=4)
+            )
+            zw = sb.tile([P, HALF], U32, name=f"zw{c}", align_bytes=64)
+            zs = sb.tile([P, HALF], U8, name=f"zs{c}", align_bytes=64)
+            nc.vector.quantize_mx(out=zw[:].bitcast(FP8X4), scales=zs[:], in_=z_bf[:].rearrange("p n t -> p (n t)"))
+            return zw, zs
+
+        def decode(acc, t, zw, zs):
+            nc.tensor.matmul_mx(
+                out=acc,
+                lhsT=dkw[:, P * t : P * (t + 1)].bitcast(FP8X4),
+                lhsT_scale=dks[:, P * t : P * (t + 1)],
+                rhs=zw[:].bitcast(FP8X4),
+                rhs_scale=zs[:],
+                start=True,
+                stop=True,
+            )
+
+        a_n1 = fetch(0, n1_t, "a_n1", "a_n1")
+        a_n2 = fetch(0, n2_t, "a_n2", "a_n2")
+        diff_a = difference(a_n1, a_n2, [0, 1, 2, 3], "diff_a", "stage")
+        b_n1 = fetch(1, n1_t, "b_n1", "b_n1")
+        weigh(0, [0, 1, 2, 3], diff_a)
+        b_n2 = fetch(1, n2_t, "b_n2", "stage")
+        zw, zs = quantised(0)
+        for t in range(PACK):
+            decode(h_first[:, t, :], t, zw, zs)
+        diff_b = difference(b_n1, b_n2, [0, 1, 2], "diff_b", "diff_b")
+        diff_b3 = difference(b_n1, b_n2, [3], "diff_b3", "diff_b3")
+        weigh(1, [0, 1, 2], diff_b)
+        weigh(1, [3], diff_b3)
+        for t in range(PACK):
+            nc.scalar.activation(h_rows[t][:, :HALF], h_first[:, t, :], ACT.Copy, scale=0.0625)
+        zw, zs = quantised(1)
+        for t in range(PACK):
+            bank = ps.tile([P, HALF], F32, name=f"h_bank{t}", tag=f"bank{t}")
+            decode(bank[:], t, zw, zs)
+            if t == 0:
+                nc.scalar.activation(h_rows[t][:, HALF:], bank[:], ACT.Copy, scale=0.0625)
+            else:
+                nc.vector.tensor_scalar(h_rows[t][:, HALF:], bank[:], 0.0625, None, ALU.mult)
+
+        out_bf = sb.tile([P, PLACES, PACK], BF16, name="out_bf", align_bytes=64)
+        out_rows = out_0.rearrange("(p t) j -> p t j", t=PACK)
+        changes = []
+        for t in range(PACK + 1):
+            if t < PACK:
+                result = sb.tile([P, PLACES], F32, name=f"result{t}")
+                old = sb.tile([P, CHANGED], F32, name=f"old{t}")
+                pa = sb.tile([P, CHANGED], F32, name=f"pa{t}")
+                nc.scalar.activation(old[:], h_rows[t][:].indirect(n3_t[:]), ACT.Copy)
+                nc.scalar.activation(pa[:], h_rows[t][:].indirect(n4_t[:]), ACT.Copy)
+                nc.vector.tensor_copy(result[:], h_rows[t][:])
+                ra = sb.tile([P, CHANGED], F32, name=f"ra{t}")
+                nc.vector.scalar_tensor_tensor(ra[:], pa[:], -0.5, old[:], ALU.mult, ALU.add)
+                changes.append((result, ra))
+            if t > 0:
+                result, ra = changes[t - 1]
+                nc.scalar.activation(result[:].indirect(n3_t[:]), ra[:], ACT.Copy)
+                nc.sync.dma_start(out_rows[:, t - 1, :], result[:])
+                nc.vector.tensor_copy(out_bf[:, :, t - 1], result[:])
+
+        ow = sb.tile([P, PLACES], U32, name="ow", align_bytes=64)
+        osc = sb.tile([P, PLACES], U8, name="osc", align_bytes=64)
+        nc.vector.quantize_mx(out=ow[:].bitcast(FP8X4), scales=osc[:], in_=out_bf[:].rearrange("p n t -> p (n t)"))
+        nc.sync.dma_start(words_of(out_1), ow[:].bitcast(I32))
+        for q in range(4):
+            queue = nc.scalar if q % 2 == 0 else nc.sync
+            queue.dma_start(out_2[0, 4 * q : 4 * q + 4, :].bitcast(I32), osc[32 * q : 32 * q + 4, :].bitcast(I32))

@@ -41,8 +41,8 @@ def tile_picked_twqjointbkdif_none_po_kernel(
             nc.sync.dma_start(t[:], src)
             return t
 
-        def zeroed_bytes(width, name, eng):
-            t = sb.tile([P, width], U8, name=name, align_bytes=64)
+        def zeroed_bytes(width, name, eng, tag=None):
+            t = sb.tile([P, width], U8, name=name, tag=tag or name, align_bytes=64)
             eng.memset(t[:].bitcast(I32), 0)
             return t
 
@@ -53,31 +53,31 @@ def tile_picked_twqjointbkdif_none_po_kernel(
         def words_of(src):
             return src[0].rearrange("p n t -> p (n t)").bitcast(I32)
 
-        w2s_raw = zeroed_bytes(FEATURES, "w2s_raw", nc.gpsimd)
         xs_tab = zeroed_bytes(TOKENS, "xs_tab", nc.vector)
-        ds_tab = zeroed_bytes(CODEWORDS, "ds_tab", nc.vector)
+        w2s_raw = zeroed_bytes(FEATURES, "w2s_raw", nc.vector, "stage")
+        ds_tab = zeroed_bytes(CODEWORDS, "ds_tab", nc.vector, "bytes")
         w1s_raw = zeroed_bytes(FEATURES, "w1s_raw", nc.vector)
 
-        load_scale_rows(xs_tab, x_scales, [nc.sync] * 4)
-        load_scale_rows(w2s_raw, w2_scales, [nc.gpsimd, nc.gpsimd, nc.sync, nc.sync])
+        w1w_raw = sb.tile([P, 2 * FEATURES], U8, name="w1w_raw", align_bytes=64)
+        nc.gpsimd.dma_start(w1w_raw[:].bitcast(I32), w1_words[0].bitcast(I32))
+        gs_t = sb.tile([P, PACK], F32, name="gs_t")
+        nc.gpsimd.dma_start(gs_t[:], gs.rearrange("(p t) o -> p (t o)", t=PACK))
         for e in range(2):
             nc.gpsimd.dma_start(ds_tab[e:P:16, :].bitcast(I32), d_scales[0, e:16:2, :].bitcast(I32))
+        load_scale_rows(xs_tab, x_scales, [nc.sync] * 4)
         two_t = load_list(two, "two_t")
+        offs_t = load_list(offs, "offs_t")
         w2w_raw = sb.tile([P, 2 * FEATURES], U8, name="w2w_raw", align_bytes=64)
         nc.sync.dma_start(w2w_raw[:].bitcast(I32), w2_words[0].bitcast(I32))
-        offs_t = load_list(offs, "offs_t")
+        xw_tab = sb.tile([P, TOKENS], U32, name="xw_tab", align_bytes=64)
+        nc.sync.dma_start(xw_tab[:].bitcast(I32), words_of(x_words))
+        load_scale_rows(w2s_raw, w2_scales, [nc.sync] * 4)
+        load_scale_rows(w1s_raw, w1_scales, [nc.sync] * 4)
         n1_t = load_list(n1, "n1_t")
         n2_t = load_list(n2, "n2_t")
         k1_t = load_list(k1, "k1_t")
-        xw_tab = sb.tile([P, TOKENS], U32, name="xw_tab", align_bytes=64)
-        nc.sync.dma_start(xw_tab[:].bitcast(I32), words_of(x_words))
-        w1w_raw = sb.tile([P, 2 * FEATURES], U8, name="w1w_raw", align_bytes=64)
-        nc.sync.dma_start(w1w_raw[:].bitcast(I32), w1_words[0].bitcast(I32))
-        dw_tab = sb.tile([P, CODEWORDS], U32, name="dw_tab", align_bytes=64)
+        dw_tab = sb.tile([P, CODEWORDS], U32, name="dw_tab", tag="table", align_bytes=64)
         nc.sync.dma_start(dw_tab[:].bitcast(I32), words_of(d_words))
-        load_scale_rows(w1s_raw, w1_scales, [nc.sync] * 4)
-        gs_t = sb.tile([P, PACK], F32, name="gs_t")
-        nc.sync.dma_start(gs_t[:], gs.rearrange("(p t) o -> p (t o)", t=PACK))
         n3_t = load_list(n3, "n3_t")
         n4_t = load_list(n4, "n4_t")
 
@@ -86,8 +86,8 @@ def tile_picked_twqjointbkdif_none_po_kernel(
             nc.vector.tensor_copy(t[:], table[:].indirect(offsets[:]))
             return t
 
-        def dealt(copy, raw, view, name):
-            t = sb.tile(list(raw[:].shape), raw[:].dtype, name=name, align_bytes=64)
+        def dealt(copy, raw, view, name, tag=None):
+            t = sb.tile(list(raw[:].shape), raw[:].dtype, name=name, tag=tag or name, align_bytes=64)
             dst, src = (t[:], raw[:]) if view is None else (t[:].bitcast(view), raw[:].bitcast(view))
             copy(dst.rearrange("p (t m) -> p m t", t=PACK), src.rearrange("p (m t) -> p m t", t=PACK))
             return t
@@ -97,72 +97,58 @@ def tile_picked_twqjointbkdif_none_po_kernel(
                 out=out,
                 lhsT=w_words[:, 2 * P * t : 2 * P * (t + 1)].bitcast(FP4X4),
                 lhsT_scale=w_scales[:, P * t : P * (t + 1)],
-                rhs=xw[:].bitcast(FP8X4),
-                rhs_scale=xs[:],
+                rhs=xw.bitcast(FP8X4),
+                rhs_scale=xs,
                 start=True,
                 stop=True,
             )
 
         xs_two = gathered(xs_tab, two_t, PLACES, U8, "xs_two")
+        xs_idx = gathered(xs_tab, offs_t, PLACES, U8, "xs_idx")
         w2w = dealt(nc.scalar.copy, w2w_raw, U16, "w2w")
         w1w = dealt(nc.scalar.copy, w1w_raw, U16, "w1w")
         xw_two = gathered(xw_tab, two_t, PLACES, U32, "xw_two")
         w2s = dealt(nc.vector.tensor_copy, w2s_raw, None, "w2s")
+        xw_idx = gathered(xw_tab, offs_t, PLACES, U32, "xw_idx")
         d_rows = []
         for t in range(PACK):
             bank = ps.tile([P, PLACES], F32, name=f"d_bank{t}", tag=f"bank{t}")
-            project(bank[:], w2w, w2s, t, xw_two, xs_two)
+            project(bank[:], w2w, w2s, t, xw_two[:], xs_two[:])
             row = sb.tile([P, PLACES], F32, name=f"d_row{t}")
             nc.scalar.activation(row[:], bank[:], ACT.Copy)
             d_rows.append(row)
 
-        xs_idx = gathered(xs_tab, offs_t, PLACES, U8, "xs_idx")
-        xw_idx = gathered(xw_tab, offs_t, PLACES, U32, "xw_idx")
-
-        ds_k1 = gathered(ds_tab, k1_t, FEATURES, U8, "ds_k1", "stage")
-        dks = dealt(nc.vector.tensor_copy, ds_k1, None, "dks")
-        for e in range(2):
-            nc.sync.dma_start(dks[2 + e : P : 32, :].bitcast(I32), dks[16 + e : P : 32, :].bitcast(I32))
 
         w1s = dealt(nc.vector.tensor_copy, w1s_raw, None, "w1s")
-        y_banks = [ps.tile([P, 2, PLACES], F32, name=f"y_bank{u}") for u in range(2)]
-        for t in range(PACK):
-            project(y_banks[t // 2][:, t % 2, :], w1w, w1s, t, xw_idx, xs_idx)
-
-        dw_k1 = gathered(dw_tab, k1_t, FEATURES, U32, "dw_k1", "stage")
-        dkw = dealt(nc.vector.tensor_copy, dw_k1, None, "dkw")
-
-        h_rows = [sb.tile([P, PLACES], F32, name=f"h_row{t}") for t in range(PACK)]
-        h_first = ps.tile([P, PACK, HALF], F32, name="h_first")
-        z_planes = [sb.tile([P, PACK, HALF], F32, name=f"z_planes{c}") for c in range(2)]
-
-        def fetch(c, offsets, name, tag):
-            entries = slice(c * HALF // LIST_ROWS, (c + 1) * HALF // LIST_ROWS)
-            picked = sb.tile([P, PACK, HALF], F32, name=name, tag=tag, align_bytes=64)
+        halves = [slice(0, HALF), slice(HALF, PLACES)]
+        y_banks = [ps.tile([P, PACK, HALF], F32, name=f"y_bank{c}") for c in range(2)]
+        for c in range(2):
             for t in range(PACK):
+                project(y_banks[c][:, t, :], w1w, w1s, t, xw_idx[:, halves[c]], xs_idx[:, halves[c]])
+
+        def fetch(picked, c, offsets, ts):
+            entries = slice(c * HALF // LIST_ROWS, (c + 1) * HALF // LIST_ROWS)
+            for t in ts:
                 nc.scalar.activation(picked[:, t, :], d_rows[t][:].indirect(offsets[:, entries]), ACT.Copy)
-            return picked
 
-        def difference(at_n1, at_n2, ts, name, tag):
-            diff = sb.tile([P, len(ts), HALF], F32, name=name, tag=tag, align_bytes=64)
-            planes = slice(ts[0], ts[-1] + 1)
-            nc.vector.tensor_tensor(diff[:], at_n1[:, planes, :], at_n2[:, planes, :], ALU.subtract)
-            return diff[:]
+        def difference(diff, at_n1, at_n2, planes):
+            nc.vector.tensor_tensor(diff[:, planes, :], at_n1[:, planes, :], at_n2[:, planes, :], ALU.subtract)
 
-        def weigh(c, ts, diff):
-            cols = slice(c * HALF, (c + 1) * HALF)
-            gate = sb.tile([P, len(ts), HALF], F32, name=f"gate{c}{ts[0]}")
-            nc.scalar.activation(gate[:], diff, ACT.Tanh)
-            for i, t in enumerate(ts):
-                nc.vector.scalar_tensor_tensor(
-                    z_planes[c][:, t, :], y_banks[t // 2][:, t % 2, cols], gs_t[:, t : t + 1], gate[:, i, :], ALU.mult, ALU.mult
-                )
-
-        def quantised(c):
-            z_bf = sb.tile([P, HALF, PACK], BF16, name=f"z_bf{c}", align_bytes=64)
-            nc.vector.tensor_copy(
-                z_bf[:].rearrange("p (a i) t -> p a t i", i=4), z_planes[c][:].rearrange("p t (a i) -> p a t i", i=4)
+        def weighted(c):
+            yg = sb.tile([P, HALF, PACK], F32, name=f"yg{c}")
+            nc.vector.tensor_tensor(
+                yg[:], y_banks[c][:].rearrange("p t j -> p j t"), gs_t[:].unsqueeze(1).broadcast_to([P, HALF, PACK]), ALU.mult
             )
+            return yg
+
+        def gated(c, diff, yg):
+            gate = sb.tile([P, HALF, PACK], F32, name=f"gate{c}", tag="last" if c == 0 else "gate", align_bytes=64)
+            nc.scalar.activation(gate[:], diff[:].rearrange("p t j -> p j t"), ACT.Tanh)
+            z_bf = sb.tile([P, HALF, PACK], BF16, name=f"z_bf{c}", tag="table" if c == 0 else "z_bf", align_bytes=64)
+            nc.vector.tensor_tensor(z_bf[:], yg[:], gate[:], ALU.mult)
+            return z_bf
+
+        def quantised(c, z_bf):
             zw = sb.tile([P, HALF], U32, name=f"zw{c}", align_bytes=64)
             zs = sb.tile([P, HALF], U8, name=f"zs{c}", align_bytes=64)
             nc.vector.quantize_mx(out=zw[:].bitcast(FP8X4), scales=zs[:], in_=z_bf[:].rearrange("p n t -> p (n t)"))
@@ -179,29 +165,48 @@ def tile_picked_twqjointbkdif_none_po_kernel(
                 stop=True,
             )
 
-        a_n1 = fetch(0, n1_t, "a_n1", "a_n1")
-        a_n2 = fetch(0, n2_t, "a_n2", "a_n2")
-        diff_a = difference(a_n1, a_n2, [0, 1, 2, 3], "diff_a", "stage")
-        b_n1 = fetch(1, n1_t, "b_n1", "b_n1")
-        weigh(0, [0, 1, 2, 3], diff_a)
-        b_n2 = fetch(1, n2_t, "b_n2", "stage")
-        zw, zs = quantised(0)
+        yg = [weighted(c) for c in range(2)]
+        ds_k1 = gathered(ds_tab, k1_t, FEATURES, U8, "ds_k1", "stage")
+
+        a_n1 = sb.tile([P, PACK, HALF], F32, name="a_n1", tag="picked")
+        a_n2 = sb.tile([P, PACK, HALF], F32, name="a_n2")
+        b_n1 = sb.tile([P, PACK, HALF], F32, name="b_n1", tag="second", align_bytes=64)
         for t in range(PACK):
-            decode(h_first[:, t, :], t, zw, zs)
-        diff_b = difference(b_n1, b_n2, [0, 1, 2], "diff_b", "diff_b")
-        diff_b3 = difference(b_n1, b_n2, [3], "diff_b3", "diff_b3")
-        weigh(1, [0, 1, 2], diff_b)
-        weigh(1, [3], diff_b3)
+            fetch(a_n1, 0, n1_t, [t])
+            fetch(a_n2, 0, n2_t, [t])
+        diff_a = sb.tile([P, PACK, HALF], F32, name="diff_a", tag="bytes", align_bytes=64)
+        difference(diff_a, a_n1, a_n2, slice(0, PACK))
+        dks = dealt(nc.vector.tensor_copy, ds_k1, None, "dks")
+        for e in range(2):
+            nc.sync.dma_start(dks[2 + e : P : 32, :].bitcast(I32), dks[16 + e : P : 32, :].bitcast(I32))
+        dw_k1 = gathered(dw_tab, k1_t, FEATURES, U32, "dw_k1")
+        fetch(b_n1, 1, n1_t, range(PACK))
+        z_a = gated(0, diff_a, yg[0])
+        b_n2 = sb.tile([P, PACK, HALF], F32, name="b_n2", tag="picked")
+        fetch(b_n2, 1, n2_t, range(PACK))
+        diff_b = sb.tile([P, PACK, HALF], F32, name="diff_b", tag="last", align_bytes=64)
+        difference(diff_b, b_n1, b_n2, slice(0, PACK - 1))
+        zw, zs = quantised(0, z_a)
+        difference(diff_b, b_n1, b_n2, slice(PACK - 1, PACK))
+        dkw = dealt(nc.vector.tensor_copy, dw_k1, None, "dkw", "second")
+        h_first = ps.tile([P, HALF], F32, name="h_first")
+        h_banks = [ps.tile([P, PLACES], F32, name=f"h_bank{t}", tag=f"bank{t}") for t in range(PACK)]
+        decode(h_first[:], 0, zw, zs)
+        for t in range(1, PACK):
+            decode(h_banks[t][:, :HALF], t, zw, zs)
+        z_b = gated(1, diff_b, yg[1])
+        h_rows = [
+            sb.tile([P, PLACES], F32, name=f"h_row{t}", tag="last" if t == 0 else f"h_row{t}", align_bytes=64)
+            for t in range(PACK)
+        ]
+        nc.scalar.activation(h_rows[0][:, :HALF], h_first[:], ACT.Copy, scale=0.0625)
+        zw, zs = quantised(1, z_b)
         for t in range(PACK):
-            nc.scalar.activation(h_rows[t][:, :HALF], h_first[:, t, :], ACT.Copy, scale=0.0625)
-        zw, zs = quantised(1)
-        for t in range(PACK):
-            bank = ps.tile([P, HALF], F32, name=f"h_bank{t}", tag=f"bank{t}")
-            decode(bank[:], t, zw, zs)
+            decode(h_banks[t][:, HALF:], t, zw, zs)
             if t == 0:
-                nc.scalar.activation(h_rows[t][:, HALF:], bank[:], ACT.Copy, scale=0.0625)
+                nc.scalar.activation(h_rows[t][:, HALF:], h_banks[t][:, HALF:], ACT.Copy, scale=0.0625)
             else:
-                nc.vector.tensor_scalar(h_rows[t][:, HALF:], bank[:], 0.0625, None, ALU.mult)
+                nc.vector.tensor_scalar(h_rows[t][:], h_banks[t][:], 0.0625, None, ALU.mult)
 
         out_bf = sb.tile([P, PLACES, PACK], BF16, name="out_bf", align_bytes=64)
         out_rows = out_0.rearrange("(p t) j -> p t j", t=PACK)
@@ -221,11 +226,15 @@ def tile_picked_twqjointbkdif_none_po_kernel(
                 result, ra = changes[t - 1]
                 nc.scalar.activation(result[:].indirect(n3_t[:]), ra[:], ACT.Copy)
                 nc.sync.dma_start(out_rows[:, t - 1, :], result[:])
-                nc.vector.tensor_copy(out_bf[:, :, t - 1], result[:])
+                for cols in halves if t == PACK else [slice(0, PLACES)]:
+                    nc.vector.tensor_copy(out_bf[:, cols, t - 1], result[:, cols])
 
         ow = sb.tile([P, PLACES], U32, name="ow", align_bytes=64)
         osc = sb.tile([P, PLACES], U8, name="osc", align_bytes=64)
-        nc.vector.quantize_mx(out=ow[:].bitcast(FP8X4), scales=osc[:], in_=out_bf[:].rearrange("p n t -> p (n t)"))
+        for cols in halves:
+            nc.vector.quantize_mx(
+                out=ow[:, cols].bitcast(FP8X4), scales=osc[:, cols], in_=out_bf[:, cols, :].rearrange("p n t -> p (n t)")
+            )
         nc.sync.dma_start(words_of(out_1), ow[:].bitcast(I32))
         for q in range(4):
             queue = nc.scalar if q % 2 == 0 else nc.sync

@@ -55,13 +55,11 @@ def tile_picked_twqjointbkdif_none_po_kernel(
 
         xs_tab = zeroed_bytes(TOKENS, "xs_tab", nc.vector)
         w2s_raw = zeroed_bytes(FEATURES, "w2s_raw", nc.vector, "stage")
-        ds_tab = zeroed_bytes(CODEWORDS, "ds_tab", nc.vector, "bytes")
+        ds_tab = zeroed_bytes(CODEWORDS, "ds_tab", nc.vector)
         w1s_raw = zeroed_bytes(FEATURES, "w1s_raw", nc.vector)
 
         w1w_raw = sb.tile([P, 2 * FEATURES], U8, name="w1w_raw", align_bytes=64)
         nc.gpsimd.dma_start(w1w_raw[:].bitcast(I32), w1_words[0].bitcast(I32))
-        gs_t = sb.tile([P, PACK], F32, name="gs_t")
-        nc.gpsimd.dma_start(gs_t[:], gs.rearrange("(p t) o -> p (t o)", t=PACK))
         for e in range(2):
             nc.gpsimd.dma_start(ds_tab[e:P:16, :].bitcast(I32), d_scales[0, e:16:2, :].bitcast(I32))
         load_scale_rows(xs_tab, x_scales, [nc.sync] * 4)
@@ -72,10 +70,12 @@ def tile_picked_twqjointbkdif_none_po_kernel(
         xw_tab = sb.tile([P, TOKENS], U32, name="xw_tab", align_bytes=64)
         nc.sync.dma_start(xw_tab[:].bitcast(I32), words_of(x_words))
         load_scale_rows(w2s_raw, w2_scales, [nc.sync] * 4)
-        load_scale_rows(w1s_raw, w1_scales, [nc.sync] * 4)
+        load_scale_rows(w1s_raw, w1_scales, [nc.sync] * 3 + [nc.gpsimd])
+        k1_t = load_list(k1, "k1_t")
+        gs_t = sb.tile([P, PACK], F32, name="gs_t")
+        nc.sync.dma_start(gs_t[:], gs.rearrange("(p t) o -> p (t o)", t=PACK))
         n1_t = load_list(n1, "n1_t")
         n2_t = load_list(n2, "n2_t")
-        k1_t = load_list(k1, "k1_t")
         dw_tab = sb.tile([P, CODEWORDS], U32, name="dw_tab", tag="table", align_bytes=64)
         nc.sync.dma_start(dw_tab[:].bitcast(I32), words_of(d_words))
         n3_t = load_list(n3, "n3_t")
@@ -165,8 +165,11 @@ def tile_picked_twqjointbkdif_none_po_kernel(
                 stop=True,
             )
 
-        yg = [weighted(c) for c in range(2)]
         ds_k1 = gathered(ds_tab, k1_t, FEATURES, U8, "ds_k1", "stage")
+        dks = dealt(nc.vector.tensor_copy, ds_k1, None, "dks")
+        for e in range(2):
+            nc.sync.dma_start(dks[2 + e : P : 32, :].bitcast(I32), dks[16 + e : P : 32, :].bitcast(I32))
+        yg = [weighted(c) for c in range(2)]
 
         a_n1 = sb.tile([P, PACK, HALF], F32, name="a_n1", tag="picked")
         a_n2 = sb.tile([P, PACK, HALF], F32, name="a_n2")
@@ -174,11 +177,8 @@ def tile_picked_twqjointbkdif_none_po_kernel(
         for t in range(PACK):
             fetch(a_n1, 0, n1_t, [t])
             fetch(a_n2, 0, n2_t, [t])
-        diff_a = sb.tile([P, PACK, HALF], F32, name="diff_a", tag="bytes", align_bytes=64)
+        diff_a = sb.tile([P, PACK, HALF], F32, name="diff_a", tag="stage", align_bytes=64)
         difference(diff_a, a_n1, a_n2, slice(0, PACK))
-        dks = dealt(nc.vector.tensor_copy, ds_k1, None, "dks")
-        for e in range(2):
-            nc.sync.dma_start(dks[2 + e : P : 32, :].bitcast(I32), dks[16 + e : P : 32, :].bitcast(I32))
         dw_k1 = gathered(dw_tab, k1_t, FEATURES, U32, "dw_k1")
         fetch(b_n1, 1, n1_t, range(PACK))
         z_a = gated(0, diff_a, yg[0])

@@ -46,9 +46,9 @@ def tile_picked_twqjointbkdif_none_po_kernel(
             eng.memset(t[:].bitcast(I32), 0)
             return t
 
-        def load_scale_rows(t, src, queues):
-            for q in range(4):
-                queues[q].dma_start(t[32 * q : 32 * q + 4, :].bitcast(I32), src[0, 4 * q : 4 * q + 4, :].bitcast(I32))
+        def load_scale_rows(t, src, queue, quadrants):
+            for q in quadrants:
+                queue.dma_start(t[32 * q : 32 * q + 4, :].bitcast(I32), src[0, 4 * q : 4 * q + 4, :].bitcast(I32))
 
         def words_of(src):
             return src[0].rearrange("p n t -> p (n t)").bitcast(I32)
@@ -60,22 +60,23 @@ def tile_picked_twqjointbkdif_none_po_kernel(
 
         w1w_raw = sb.tile([P, 2 * FEATURES], U8, name="w1w_raw", align_bytes=64)
         nc.gpsimd.dma_start(w1w_raw[:].bitcast(I32), w1_words[0].bitcast(I32))
+        load_scale_rows(w2s_raw, w2_scales, nc.gpsimd, [3])
         for e in range(2):
             nc.gpsimd.dma_start(ds_tab[e:P:16, :].bitcast(I32), d_scales[0, e:16:2, :].bitcast(I32))
-        load_scale_rows(xs_tab, x_scales, [nc.sync] * 4)
+        load_scale_rows(xs_tab, x_scales, nc.sync, range(4))
         two_t = load_list(two, "two_t")
         offs_t = load_list(offs, "offs_t")
         w2w_raw = sb.tile([P, 2 * FEATURES], U8, name="w2w_raw", align_bytes=64)
         nc.sync.dma_start(w2w_raw[:].bitcast(I32), w2_words[0].bitcast(I32))
         xw_tab = sb.tile([P, TOKENS], U32, name="xw_tab", align_bytes=64)
         nc.sync.dma_start(xw_tab[:].bitcast(I32), words_of(x_words))
-        load_scale_rows(w2s_raw, w2_scales, [nc.sync] * 4)
-        load_scale_rows(w1s_raw, w1_scales, [nc.sync] * 3 + [nc.gpsimd])
+        load_scale_rows(w2s_raw, w2_scales, nc.sync, range(3))
+        load_scale_rows(w1s_raw, w1_scales, nc.sync, range(4))
         k1_t = load_list(k1, "k1_t")
-        gs_t = sb.tile([P, PACK], F32, name="gs_t")
-        nc.sync.dma_start(gs_t[:], gs.rearrange("(p t) o -> p (t o)", t=PACK))
         n1_t = load_list(n1, "n1_t")
         n2_t = load_list(n2, "n2_t")
+        gs_t = sb.tile([P, PACK], F32, name="gs_t")
+        nc.sync.dma_start(gs_t[:], gs.rearrange("(p t) o -> p (t o)", t=PACK))
         dw_tab = sb.tile([P, CODEWORDS], U32, name="dw_tab", tag="table", align_bytes=64)
         nc.sync.dma_start(dw_tab[:].bitcast(I32), words_of(d_words))
         n3_t = load_list(n3, "n3_t")
@@ -141,11 +142,13 @@ def tile_picked_twqjointbkdif_none_po_kernel(
             )
             return yg
 
-        def gated(c, diff, yg):
+        def gated(c, diff, yg, pieces):
             gate = sb.tile([P, HALF, PACK], F32, name=f"gate{c}", tag="last" if c == 0 else "gate", align_bytes=64)
-            nc.scalar.activation(gate[:], diff[:].rearrange("p t j -> p j t"), ACT.Tanh)
             z_bf = sb.tile([P, HALF, PACK], BF16, name=f"z_bf{c}", tag="table" if c == 0 else "z_bf", align_bytes=64)
-            nc.vector.tensor_tensor(z_bf[:], yg[:], gate[:], ALU.mult)
+            for i in range(pieces):
+                cols = slice(i * HALF // pieces, (i + 1) * HALF // pieces)
+                nc.scalar.activation(gate[:, cols, :], diff[:, :, cols].rearrange("p t j -> p j t"), ACT.Tanh)
+                nc.vector.tensor_tensor(z_bf[:, cols, :], yg[:, cols, :], gate[:, cols, :], ALU.mult)
             return z_bf
 
         def quantised(c, z_bf):
@@ -181,20 +184,20 @@ def tile_picked_twqjointbkdif_none_po_kernel(
         difference(diff_a, a_n1, a_n2, slice(0, PACK))
         dw_k1 = gathered(dw_tab, k1_t, FEATURES, U32, "dw_k1")
         fetch(b_n1, 1, n1_t, range(PACK))
-        z_a = gated(0, diff_a, yg[0])
+        z_a = gated(0, diff_a, yg[0], 1)
         b_n2 = sb.tile([P, PACK, HALF], F32, name="b_n2", tag="picked")
         fetch(b_n2, 1, n2_t, range(PACK))
         diff_b = sb.tile([P, PACK, HALF], F32, name="diff_b", tag="last", align_bytes=64)
         difference(diff_b, b_n1, b_n2, slice(0, PACK - 1))
-        zw, zs = quantised(0, z_a)
         difference(diff_b, b_n1, b_n2, slice(PACK - 1, PACK))
+        zw, zs = quantised(0, z_a)
         dkw = dealt(nc.vector.tensor_copy, dw_k1, None, "dkw", "second")
         h_first = ps.tile([P, HALF], F32, name="h_first")
         h_banks = [ps.tile([P, PLACES], F32, name=f"h_bank{t}", tag=f"bank{t}") for t in range(PACK)]
         decode(h_first[:], 0, zw, zs)
         for t in range(1, PACK):
             decode(h_banks[t][:, :HALF], t, zw, zs)
-        z_b = gated(1, diff_b, yg[1])
+        z_b = gated(1, diff_b, yg[1], 2)
         h_rows = [
             sb.tile([P, PLACES], F32, name=f"h_row{t}", tag="last" if t == 0 else f"h_row{t}", align_bytes=64)
             for t in range(PACK)

from contextlib import ExitStack

import concourse.mybir as mybir

F32 = mybir.dt.float32
BF16 = mybir.dt.bfloat16
I32 = mybir.dt.int32
U32 = mybir.dt.uint32
U16 = mybir.dt.uint16
U8 = mybir.dt.uint8
FP8X4 = mybir.dt.float8_e4m3fn_x4
FP4X4 = mybir.dt.float4_e2m1fn_x4
ACT = mybir.ActivationFunctionType
ALU = mybir.AluOpType

P = 128
PACK = 4
TOKENS = 1024
CODEWORDS = 2048
FEATURES = 512
PLACES = 256
CHANGED = 192
HALF = PLACES // 2
LIST_ROWS = 16

FLOPS = 3 * 2 * FEATURES * FEATURES * PLACES


def tile_picked_twqjointbkdif_none_po_kernel(
    tc, x_words, x_scales, w1_words, w1_scales, w2_words, w2_scales, gs, d_words, d_scales,
    offs, two, n1, n2, k1, n3, n4, out_0, out_1, out_2,
):
    nc = tc.nc
    with ExitStack() as ctx:
        lists = ctx.enter_context(tc.tile_pool(name="lists", bufs=1))
        sb = ctx.enter_context(tc.tile_pool(name="sb", bufs=1))
        ps = ctx.enter_context(tc.psum_pool(name="ps", bufs=1))

        def load_list(src, name):
            t = lists.tile(list(src.shape), U16, name=name)
            nc.sync.dma_start(t[:], src)
            return t

        def zeroed_bytes(width, name, eng, tag=None):
            t = sb.tile([P, width], U8, name=name, tag=tag or name, align_bytes=64)
            eng.memset(t[:].bitcast(I32), 0)
            return t

        def load_scale_rows(t, src, queue, quadrants):
            for q in quadrants:
                queue.dma_start(t[32 * q : 32 * q + 4, :].bitcast(I32), src[0, 4 * q : 4 * q + 4, :].bitcast(I32))

        def words_of(src):
            return src[0].rearrange("p n t -> p (n t)").bitcast(I32)

        xs_tab = zeroed_bytes(TOKENS, "xs_tab", nc.vector)
        w2s_raw = zeroed_bytes(FEATURES, "w2s_raw", nc.vector, "stage")
        ds_tab = zeroed_bytes(CODEWORDS, "ds_tab", nc.vector)
        w1s_raw = zeroed_bytes(FEATURES, "w1s_raw", nc.vector)

        w1w_raw = sb.tile([P, 2 * FEATURES], U8, name="w1w_raw", align_bytes=64)
        nc.gpsimd.dma_start(w1w_raw[:].bitcast(I32), w1_words[0].bitcast(I32))
        load_scale_rows(w2s_raw, w2_scales, nc.gpsimd, [3])
        for e in range(2):
            nc.gpsimd.dma_start(ds_tab[e:P:16, :].bitcast(I32), d_scales[0, e:16:2, :].bitcast(I32))
        load_scale_rows(xs_tab, x_scales, nc.sync, range(4))
        two_t = load_list(two, "two_t")
        offs_t = load_list(offs, "offs_t")
        w2w_raw = sb.tile([P, 2 * FEATURES], U8, name="w2w_raw", align_bytes=64)
        nc.sync.dma_start(w2w_raw[:].bitcast(I32), w2_words[0].bitcast(I32))
        xw_tab = sb.tile([P, TOKENS], U32, name="xw_tab", align_bytes=64)
        nc.sync.dma_start(xw_tab[:].bitcast(I32), words_of(x_words))
        load_scale_rows(w2s_raw, w2_scales, nc.sync, range(3))
        load_scale_rows(w1s_raw, w1_scales, nc.sync, range(4))
        k1_t = load_list(k1, "k1_t")
        n1_t = load_list(n1, "n1_t")
        n2_t = load_list(n2, "n2_t")
        gs_t = sb.tile([P, PACK], F32, name="gs_t")
        nc.sync.dma_start(gs_t[:], gs.rearrange("(p t) o -> p (t o)", t=PACK))
        dw_tab = sb.tile([P, CODEWORDS], U32, name="dw_tab", tag="table", align_bytes=64)
        nc.sync.dma_start(dw_tab[:].bitcast(I32), words_of(d_words))
        n3_t = load_list(n3, "n3_t")
        n4_t = load_list(n4, "n4_t")

        def gathered(table, offsets, n, dtype, name, tag=None):
            t = sb.tile([P, n], dtype, name=name, tag=tag or name, align_bytes=64)
            nc.vector.tensor_copy(t[:], table[:].indirect(offsets[:]))
            return t

        def dealt(copy, raw, view, name, tag=None):
            t = sb.tile(list(raw[:].shape), raw[:].dtype, name=name, tag=tag or name, align_bytes=64)
            dst, src = (t[:], raw[:]) if view is None else (t[:].bitcast(view), raw[:].bitcast(view))
            copy(dst.rearrange("p (t m) -> p m t", t=PACK), src.rearrange("p (m t) -> p m t", t=PACK))
            return t

        def project(out, w_words, w_scales, t, xw, xs):
            nc.tensor.matmul_mx(
                out=out,
                lhsT=w_words[:, 2 * P * t : 2 * P * (t + 1)].bitcast(FP4X4),
                lhsT_scale=w_scales[:, P * t : P * (t + 1)],
                rhs=xw.bitcast(FP8X4),
                rhs_scale=xs,
                start=True,
                stop=True,
            )

        xs_two = gathered(xs_tab, two_t, PLACES, U8, "xs_two")
        xs_idx = gathered(xs_tab, offs_t, PLACES, U8, "xs_idx")
        w2w = dealt(nc.scalar.copy, w2w_raw, U16, "w2w")
        w1w = dealt(nc.scalar.copy, w1w_raw, U16, "w1w")
        xw_two = gathered(xw_tab, two_t, PLACES, U32, "xw_two")
        w2s = dealt(nc.vector.tensor_copy, w2s_raw, None, "w2s")
        xw_idx = gathered(xw_tab, offs_t, PLACES, U32, "xw_idx")
        d_rows = []
        for t in range(PACK):
            bank = ps.tile([P, PLACES], F32, name=f"d_bank{t}", tag=f"bank{t}")
            project(bank[:], w2w, w2s, t, xw_two[:], xs_two[:])
            row = sb.tile([P, PLACES], F32, name=f"d_row{t}")
            nc.scalar.activation(row[:], bank[:], ACT.Copy)
            d_rows.append(row)


        w1s = dealt(nc.vector.tensor_copy, w1s_raw, None, "w1s")
        halves = [slice(0, HALF), slice(HALF, PLACES)]
        y_banks = [ps.tile([P, PACK, HALF], F32, name=f"y_bank{c}") for c in range(2)]
        for c in range(2):
            for t in range(PACK):
                project(y_banks[c][:, t, :], w1w, w1s, t, xw_idx[:, halves[c]], xs_idx[:, halves[c]])

        def fetch(picked, c, offsets, ts):
            entries = slice(c * HALF // LIST_ROWS, (c + 1) * HALF // LIST_ROWS)
            for t in ts:
                nc.scalar.activation(picked[:, t, :], d_rows[t][:].indirect(offsets[:, entries]), ACT.Copy)

        def difference(diff, at_n1, at_n2, planes):
            nc.vector.tensor_tensor(diff[:, planes, :], at_n1[:, planes, :], at_n2[:, planes, :], ALU.subtract)

        def weighted(c):
            yg = sb.tile([P, HALF, PACK], F32, name=f"yg{c}")
            nc.vector.tensor_tensor(
                yg[:], y_banks[c][:].rearrange("p t j -> p j t"), gs_t[:].unsqueeze(1).broadcast_to([P, HALF, PACK]), ALU.mult
            )
            return yg

        def gated(c, diff, yg, pieces):
            gate = sb.tile([P, HALF, PACK], F32, name=f"gate{c}", tag="last" if c == 0 else "gate", align_bytes=64)
            z_bf = sb.tile([P, HALF, PACK], BF16, name=f"z_bf{c}", tag="table" if c == 0 else "z_bf", align_bytes=64)
            for i in range(pieces):
                cols = slice(i * HALF // pieces, (i + 1) * HALF // pieces)
                nc.scalar.activation(gate[:, cols, :], diff[:, :, cols].rearrange("p t j -> p j t"), ACT.Tanh)
                nc.vector.tensor_tensor(z_bf[:, cols, :], yg[:, cols, :], gate[:, cols, :], ALU.mult)
            return z_bf

        def quantised(c, z_bf):
            zw = sb.tile([P, HALF], U32, name=f"zw{c}", align_bytes=64)
            zs = sb.tile([P, HALF], U8, name=f"zs{c}", align_bytes=64)
            nc.vector.quantize_mx(out=zw[:].bitcast(FP8X4), scales=zs[:], in_=z_bf[:].rearrange("p n t -> p (n t)"))
            return zw, zs

        def decode(acc, t, zw, zs):
            nc.tensor.matmul_mx(
                out=acc,
                lhsT=dkw[:, P * t : P * (t + 1)].bitcast(FP8X4),
                lhsT_scale=dks[:, P * t : P * (t + 1)],
                rhs=zw[:].bitcast(FP8X4),
                rhs_scale=zs[:],
                start=True,
                stop=True,
            )

        ds_k1 = gathered(ds_tab, k1_t, FEATURES, U8, "ds_k1", "stage")
        dks = dealt(nc.vector.tensor_copy, ds_k1, None, "dks")
        for e in range(2):
            nc.sync.dma_start(dks[2 + e : P : 32, :].bitcast(I32), dks[16 + e : P : 32, :].bitcast(I32))
        yg = [weighted(c) for c in range(2)]

        a_n1 = sb.tile([P, PACK, HALF], F32, name="a_n1", tag="picked")
        a_n2 = sb.tile([P, PACK, HALF], F32, name="a_n2")
        b_n1 = sb.tile([P, PACK, HALF], F32, name="b_n1", tag="second", align_bytes=64)
        for t in range(PACK):
            fetch(a_n1, 0, n1_t, [t])
            fetch(a_n2, 0, n2_t, [t])
        diff_a = sb.tile([P, PACK, HALF], F32, name="diff_a", tag="stage", align_bytes=64)
        difference(diff_a, a_n1, a_n2, slice(0, PACK))
        dw_k1 = gathered(dw_tab, k1_t, FEATURES, U32, "dw_k1")
        fetch(b_n1, 1, n1_t, range(PACK))
        z_a = gated(0, diff_a, yg[0], 1)
        b_n2 = sb.tile([P, PACK, HALF], F32, name="b_n2", tag="picked")
        fetch(b_n2, 1, n2_t, range(PACK))
        diff_b = sb.tile([P, PACK, HALF], F32, name="diff_b", tag="last", align_bytes=64)
        difference(diff_b, b_n1, b_n2, slice(0, PACK - 1))
        difference(diff_b, b_n1, b_n2, slice(PACK - 1, PACK))
        zw, zs = quantised(0, z_a)
        dkw = dealt(nc.vector.tensor_copy, dw_k1, None, "dkw", "second")
        h_first = ps.tile([P, HALF], F32, name="h_first")
        h_banks = [ps.tile([P, PLACES], F32, name=f"h_bank{t}", tag=f"bank{t}") for t in range(PACK)]
        decode(h_first[:], 0, zw, zs)
        for t in range(1, PACK):
            decode(h_banks[t][:, :HALF], t, zw, zs)
        z_b = gated(1, diff_b, yg[1], 2)
        h_rows = [
            sb.tile([P, PLACES], F32, name=f"h_row{t}", tag="last" if t == 0 else f"h_row{t}", align_bytes=64)
            for t in range(PACK)
        ]
        nc.scalar.activation(h_rows[0][:, :HALF], h_first[:], ACT.Copy, scale=0.0625)
        zw, zs = quantised(1, z_b)
        for t in range(PACK):
            decode(h_banks[t][:, HALF:], t, zw, zs)
            if t == 0:
                nc.scalar.activation(h_rows[t][:, HALF:], h_banks[t][:, HALF:], ACT.Copy, scale=0.0625)
            else:
                nc.vector.tensor_scalar(h_rows[t][:], h_banks[t][:], 0.0625, None, ALU.mult)

        out_bf = sb.tile([P, PLACES, PACK], BF16, name="out_bf", align_bytes=64)
        out_rows = out_0.rearrange("(p t) j -> p t j", t=PACK)
        changes = []
        for t in range(PACK + 1):
            if t < PACK:
                result = sb.tile([P, PLACES], F32, name=f"result{t}")
                old = sb.tile([P, CHANGED], F32, name=f"old{t}")
                pa = sb.tile([P, CHANGED], F32, name=f"pa{t}")
                nc.scalar.activation(old[:], h_rows[t][:].indirect(n3_t[:]), ACT.Copy)
                nc.scalar.activation(pa[:], h_rows[t][:].indirect(n4_t[:]), ACT.Copy)
                nc.vector.tensor_copy(result[:], h_rows[t][:])
                ra = sb.tile([P, CHANGED], F32, name=f"ra{t}")
                nc.vector.scalar_tensor_tensor(ra[:], pa[:], -0.5, old[:], ALU.mult, ALU.add)
                changes.append((result, ra))
            if t > 0:
                result, ra = changes[t - 1]
                nc.scalar.activation(result[:].indirect(n3_t[:]), ra[:], ACT.Copy)
                nc.sync.dma_start(out_rows[:, t - 1, :], result[:])
                for cols in halves if t == PACK else [slice(0, PLACES)]:
                    nc.vector.tensor_copy(out_bf[:, cols, t - 1], result[:, cols])

        ow = sb.tile([P, PLACES], U32, name="ow", align_bytes=64)
        osc = sb.tile([P, PLACES], U8, name="osc", align_bytes=64)
        for cols in halves:
            nc.vector.quantize_mx(
                out=ow[:, cols].bitcast(FP8X4), scales=osc[:, cols], in_=out_bf[:, cols, :].rearrange("p n t -> p (n t)")
            )
        nc.sync.dma_start(words_of(out_1), ow[:].bitcast(I32))
        for q in range(4):
            queue = nc.scalar if q % 2 == 0 else nc.sync
            queue.dma_start(out_2[0, 4 * q : 4 * q + 4, :].bitcast(I32), osc[32 * q : 32 * q + 4, :].bitcast(I32))
